import numpy as np
import ml_dtypes


def mxq(x, axis, fmt="e4m3"):
    dtype, down = {"e4m3": (ml_dtypes.float8_e4m3fn, 7), "e5m2": (ml_dtypes.float8_e5m2, 14)}[fmt]
    v = np.moveaxis(np.asarray(x, np.float32).astype(ml_dtypes.bfloat16).astype(np.float64), axis, -1)
    blocks = v.reshape(v.shape[:-1] + (-1, 32))
    amax = np.abs(blocks).max(-1, keepdims=True)
    byte = np.maximum(np.where(amax > 0, np.frexp(amax)[1] - 1 + 127, 0) - down, 1)
    scale = np.exp2(byte - 127.0)
    codes = (blocks / scale).astype(np.float32).astype(dtype).astype(np.float64)
    return np.moveaxis((codes * scale).reshape(v.shape), -1, axis)


WIDE = False


def mx_kscale(k):
    if not WIDE:
        return np.ones(k)
    levels = np.array([10, -10, 5, -5, 0])
    if k % 512:
        return np.exp2(np.random.permutation(np.resize(levels, k // 32))).repeat(32)
    a = np.empty((k // 512, 16))
    for p in range(k // 512):
        a[p, :8] = np.random.permutation(np.resize(levels, 8))
        for g in range(8):
            far = levels[np.abs(levels - a[p, g]) >= 10]
            a[p, g + 8] = far[np.random.randint(len(far))]
    return np.exp2(a.ravel()).repeat(32)


def f64(x):
    return np.asarray(x).astype(np.float64)


def striped(idx):
    return np.tile(idx.reshape(-1, 16).T, (8, 1)).astype(np.uint16)


def unstriped(offs):
    return offs[:16].T.reshape(-1).astype(np.int64)


K, T, S, N = 1024, 2048, 512, 256


def setup_inputs():
    n = np.random.standard_normal
    s = mx_kscale(K)[:, None]
    return {
        "xT": (n((K, T)) * s).astype(np.float32),
        "w1": (n((K, N)) / np.sqrt(K) / s).astype(np.float32),
        "w2": (n((K, N)) / np.sqrt(K) / s).astype(np.float32),
        "w3": (n((K, N)) / np.sqrt(K) / s).astype(np.float32),
        "offs": striped(np.random.permutation(T)[:S]),
    }


def reference(xT, w1, w2, w3, offs):
    xq = mxq(f64(xT)[:, unstriped(offs)], 0, "e4m3")
    return np.maximum(np.maximum(mxq(f64(w1), 0, "e4m3").T @ xq, mxq(f64(w2), 0, "e4m3").T @ xq), mxq(f64(w3), 0, "e4m3").T @ xq)

@@ -1,0 +1,117 @@
+from contextlib import ExitStack
+
+import concourse.mybir as mybir
+
+K, T, S, N = 1024, 2048, 512, 256
+FLOPS = 3 * 2 * K * N * S
+
+F32 = mybir.dt.float32
+BF16 = mybir.dt.bfloat16
+U32 = mybir.dt.uint32
+U16 = mybir.dt.uint16
+U8 = mybir.dt.uint8
+FP8X4 = mybir.dt.float8_e4m3fn_x4
+MAX = mybir.AluOpType.max
+
+P = 128
+PACK = 4
+KP = P * PACK
+PASSES = K // KP
+
+
+def tile_picked_maxout_max_e_kernel(tc, xT, w1, w2, w3, offs, out):
+    nc = tc.nc
+    ws = (w1, w2, w3)
+    with ExitStack() as ctx:
+        keep = ctx.enter_context(tc.tile_pool(name="keep", bufs=1))
+        psum = ctx.enter_context(tc.psum_pool(name="psum", bufs=1))
+
+        offsets = keep.tile([P, S // 16], U16, name="offsets")
+        x_rows = xT.rearrange("(g p j) t -> g j p t", p=P, j=PACK)
+        planes = {}
+        for g in range(PASSES):
+            for j in range(PACK):
+                planes[g, j] = keep.tile([P, T], F32, name=f"x_{g}_{j}")
+                nc.sync.dma_start(out=planes[g, j][:], in_=x_rows[g, j])
+                if (g, j) == (0, 0):
+                    nc.sync.dma_start(offsets[:], offs)
+
+        raw = {}
+        for m in range(2):
+            for i in range(3):
+                for g in range(PASSES):
+                    raw[i, m, g] = keep.tile([P, PACK, P], F32, name=f"wraw_{i}_{m}_{g}")
+                    nc.sync.dma_start(
+                        out=raw[i, m, g][:],
+                        in_=ws[i][g * KP : (g + 1) * KP, m * P : (m + 1) * P].rearrange("(p j) n -> p j n", j=PACK),
+                    )
+
+        x_codes, x_scales = {}, {}
+        for g in range(PASSES):
+            picked = keep.tile([P, S, PACK], BF16, name=f"picked_{g}", align_bytes=64)
+            for j in range(PACK):
+                nc.vector.tensor_copy(out=picked[:, :, j], in_=planes[g, j][:].indirect(offsets[:]))
+            x_codes[g] = keep.tile([P, S], U32, name=f"x_codes_{g}", align_bytes=64)
+            x_scales[g] = keep.tile([P, S], U8, name=f"x_scales_{g}", align_bytes=64)
+            nc.vector.quantize_mx(
+                out=x_codes[g][:].bitcast(FP8X4), scales=x_scales[g][:], in_=picked[:].rearrange("p s j -> p (s j)")
+            )
+
+        grouped, w_codes, w_scales, acc, best = {}, {}, {}, {}, {}
+
+        def weave(i, m, g, on_vector):
+            grouped[i, m, g] = keep.tile([P, P, PACK], BF16, name=f"wg_{i}_{m}_{g}", align_bytes=64)
+            dst = grouped[i, m, g][:].rearrange("p (c u) j -> p c j u", u=4)
+            src = raw[i, m, g][:].rearrange("p j (c u) -> p c j u", u=4)
+            if on_vector:
+                nc.vector.tensor_copy(out=dst, in_=src)
+            else:
+                nc.scalar.copy(out=dst, in_=src)
+
+        def quant(i, m, g):
+            w_codes[i, m, g] = keep.tile([P, P], U32, name=f"wc_{i}_{m}_{g}", align_bytes=64)
+            w_scales[i, m, g] = keep.tile([P, P], U8, name=f"wsc_{i}_{m}_{g}", align_bytes=64)
+            nc.vector.quantize_mx(
+                out=w_codes[i, m, g][:].bitcast(FP8X4),
+                scales=w_scales[i, m, g][:],
+                in_=grouped[i, m, g][:].rearrange("p n j -> p (n j)"),
+            )
+
+        def spans(i, m):
+            return [(0, S // 2), (S // 2, S)] if (i, m) == (2, 1) else [(0, S)]
+
+        def multiply(i, m, g):
+            for a, b in spans(i, m):
+                if g == 0:
+                    acc[i, m, a] = psum.tile([P, b - a], F32, name=f"acc_{i}_{m}_{a}")
+                nc.tensor.matmul_mx(
+                    out=acc[i, m, a][:],
+                    lhsT=w_codes[i, m, g][:].bitcast(FP8X4),
+                    lhsT_scale=w_scales[i, m, g][:],
+                    rhs=x_codes[g][:, a:b].bitcast(FP8X4),
+                    rhs_scale=x_scales[g][:, a:b],
+                    start=(g == 0),
+                    stop=(g == PASSES - 1),
+                )
+
+        def fold(i, m):
+            for a, b in spans(i, m):
+                new = keep.tile([P, b - a], F32, name=f"best_{i}_{m}_{a}")
+                if i == 0:
+                    nc.scalar.copy(out=new[:], in_=acc[i, m, a][:])
+                else:
+                    nc.vector.tensor_tensor(out=new[:], in0=acc[i, m, a][:], in1=best[i - 1, m][:, a:b], op=MAX)
+                if i == 2:
+                    nc.sync.dma_start(out=out[m * P : (m + 1) * P, a:b], in_=new[:])
+                else:
+                    best[i, m] = new
+
+        on_vector = {(2, 0, 0), (2, 0, 1), (1, 1, 0), (1, 1, 1), (2, 1, 1)}
+        for m in range(2):
+            for i in range(3):
+                for g in range(PASSES):
+                    weave(i, m, g, (i, m, g) in on_vector)
+                for g in range(PASSES):
+                    quant(i, m, g)
+                    multiply(i, m, g)
+                fold(i, m)

@@ -26,68 +26,91 @@ def tile_picked_maxout_max_e_kernel(tc, xT, w1, w2, w3, offs, out):
         keep = ctx.enter_context(tc.tile_pool(name="keep", bufs=1))
         psum = ctx.enter_context(tc.psum_pool(name="psum", bufs=1))
 
+        reuse = {"best_1_1_0":"wraw_2_1_0","best_1_0_0":"wg_2_0_0","best_2_0_256":"wg_2_1_1","x_codes_0":"x_1_0"}
+
+        def new_tile(shape, dtype, name):
+            return keep.tile(shape, dtype, name=name, tag=reuse.get(name, name), align_bytes=64)
+
         offsets = keep.tile([P, S // 16], U16, name="offsets")
-        x_rows = xT.rearrange("(g p j) t -> g j p t", p=P, j=PACK)
+        x_rows = xT.rearrange("(g p j) t -> g p j t", p=P, j=PACK)
         planes = {}
-        for g in range(PASSES):
-            for j in range(PACK):
-                planes[g, j] = keep.tile([P, T], F32, name=f"x_{g}_{j}")
-                nc.sync.dma_start(out=planes[g, j][:], in_=x_rows[g, j])
-                if (g, j) == (0, 0):
-                    nc.sync.dma_start(offsets[:], offs)
-
         raw = {}
-        for m in range(2):
-            for i in range(3):
-                for g in range(PASSES):
-                    raw[i, m, g] = keep.tile([P, PACK, P], F32, name=f"wraw_{i}_{m}_{g}")
-                    nc.sync.dma_start(
-                        out=raw[i, m, g][:],
-                        in_=ws[i][g * KP : (g + 1) * KP, m * P : (m + 1) * P].rearrange("(p j) n -> p j n", j=PACK),
-                    )
 
-        x_codes, x_scales = {}, {}
-        for g in range(PASSES):
-            picked = keep.tile([P, S, PACK], BF16, name=f"picked_{g}", align_bytes=64)
-            for j in range(PACK):
-                nc.vector.tensor_copy(out=picked[:, :, j], in_=planes[g, j][:].indirect(offsets[:]))
-            x_codes[g] = keep.tile([P, S], U32, name=f"x_codes_{g}", align_bytes=64)
-            x_scales[g] = keep.tile([P, S], U8, name=f"x_scales_{g}", align_bytes=64)
-            nc.vector.quantize_mx(
-                out=x_codes[g][:].bitcast(FP8X4), scales=x_scales[g][:], in_=picked[:].rearrange("p s j -> p (s j)")
+        def load_x(g, j0, j1):
+            rows = new_tile([P, (j1 - j0) * T], F32, f"x_{g}_{j0}")
+            nc.sync.dma_start(out=rows[:], in_=x_rows[g][:, j0:j1, :].rearrange("p j t -> p (j t)"))
+            for j in range(j0, j1):
+                planes[g, j] = rows[:, (j - j0) * T : (j - j0 + 1) * T]
+
+        def load_w(i, g):
+            rows = new_tile([P, PACK, N], F32, f"wraw_{i}_{g}")
+            nc.sync.dma_start(out=rows[:], in_=ws[i][g * KP : (g + 1) * KP, :].rearrange("(p j) n -> p j n", j=PACK))
+            for m in range(2):
+                raw[i, g, m] = rows[:, :, m * P : (m + 1) * P]
+
+        def load_w_half(i, g, m):
+            rows = new_tile([P, PACK, P], F32, f"wraw_{i}_{g}_{m}")
+            nc.sync.dma_start(
+                out=rows[:], in_=ws[i][g * KP : (g + 1) * KP, m * P : (m + 1) * P].rearrange("(p j) n -> p j n", j=PACK)
             )
+            raw[i, g, m] = rows[:]
 
+        picked, x_codes, x_scales = {}, {}, {}
         grouped, w_codes, w_scales, acc, best = {}, {}, {}, {}, {}
 
-        def weave(i, m, g, on_vector):
-            grouped[i, m, g] = keep.tile([P, P, PACK], BF16, name=f"wg_{i}_{m}_{g}", align_bytes=64)
-            dst = grouped[i, m, g][:].rearrange("p (c u) j -> p c j u", u=4)
-            src = raw[i, m, g][:].rearrange("p j (c u) -> p c j u", u=4)
+        def gather(g, j):
+            if j == 0:
+                picked[g] = new_tile([P, S, PACK], BF16, f"picked_{g}")
+            nc.vector.tensor_copy(out=picked[g][:, :, j], in_=planes[g, j].indirect(offsets[:]))
+
+        dense = new_tile([P, PACK, S], F32, "dense")
+
+        def gather_dense(j):
+            nc.vector.tensor_copy(out=dense[:, j, :], in_=planes[0, j].indirect(offsets[:]))
+
+        def weave_dense():
+            picked[0] = new_tile([P, S, PACK], BF16, "picked_0")
+            nc.scalar.copy(
+                out=picked[0][:].rearrange("p (c u) j -> p c j u", u=4),
+                in_=dense[:].rearrange("p j (c u) -> p c j u", u=4),
+            )
+
+        def quant_x(g):
+            x_codes[g] = new_tile([P, S], U32, f"x_codes_{g}")
+            x_scales[g] = new_tile([P, S], U8, f"x_scales_{g}")
+            nc.vector.quantize_mx(
+                out=x_codes[g][:].bitcast(FP8X4), scales=x_scales[g][:], in_=picked[g][:].rearrange("p s j -> p (s j)")
+            )
+
+        def weave(i, g, m, on_vector):
+            grouped[i, g, m] = new_tile([P, P, PACK], BF16, f"wg_{i}_{g}_{m}")
+            dst = grouped[i, g, m][:].rearrange("p (c u) j -> p c j u", u=4)
+            src = raw[i, g, m].rearrange("p j (c u) -> p c j u", u=4)
             if on_vector:
                 nc.vector.tensor_copy(out=dst, in_=src)
             else:
                 nc.scalar.copy(out=dst, in_=src)
 
-        def quant(i, m, g):
-            w_codes[i, m, g] = keep.tile([P, P], U32, name=f"wc_{i}_{m}_{g}", align_bytes=64)
-            w_scales[i, m, g] = keep.tile([P, P], U8, name=f"wsc_{i}_{m}_{g}", align_bytes=64)
+        def quant(i, g, m):
+            w_codes[i, g, m] = new_tile([P, P], U32, f"wc_{i}_{g}_{m}")
+            w_scales[i, g, m] = new_tile([P, P], U8, f"wsc_{i}_{g}_{m}")
             nc.vector.quantize_mx(
-                out=w_codes[i, m, g][:].bitcast(FP8X4),
-                scales=w_scales[i, m, g][:],
-                in_=grouped[i, m, g][:].rearrange("p n j -> p (n j)"),
+                out=w_codes[i, g, m][:].bitcast(FP8X4),
+                scales=w_scales[i, g, m][:],
+                in_=grouped[i, g, m][:].rearrange("p n j -> p (n j)"),
             )
 
         def spans(i, m):
-            return [(0, S // 2), (S // 2, S)] if (i, m) == (2, 1) else [(0, S)]
+            return [(0, S // 2), (S // 2, S)] if i == 2 else [(0, S)]
 
-        def multiply(i, m, g):
+        def multiply(i, g, m):
             for a, b in spans(i, m):
                 if g == 0:
                     acc[i, m, a] = psum.tile([P, b - a], F32, name=f"acc_{i}_{m}_{a}")
                 nc.tensor.matmul_mx(
                     out=acc[i, m, a][:],
-                    lhsT=w_codes[i, m, g][:].bitcast(FP8X4),
-                    lhsT_scale=w_scales[i, m, g][:],
+                    lhsT=w_codes[i, g, m][:].bitcast(FP8X4),
+                    lhsT_scale=w_scales[i, g, m][:],
                     rhs=x_codes[g][:, a:b].bitcast(FP8X4),
                     rhs_scale=x_scales[g][:, a:b],
                     start=(g == 0),
@@ -96,7 +119,7 @@ def tile_picked_maxout_max_e_kernel(tc, xT, w1, w2, w3, offs, out):
 
         def fold(i, m):
             for a, b in spans(i, m):
-                new = keep.tile([P, b - a], F32, name=f"best_{i}_{m}_{a}")
+                new = new_tile([P, b - a], F32, f"best_{i}_{m}_{a}")
                 if i == 0:
                     nc.scalar.copy(out=new[:], in_=acc[i, m, a][:])
                 else:
@@ -106,12 +129,72 @@ def tile_picked_maxout_max_e_kernel(tc, xT, w1, w2, w3, offs, out):
                 else:
                     best[i, m] = new
 
-        on_vector = {(2, 0, 0), (2, 0, 1), (1, 1, 0), (1, 1, 1), (2, 1, 1)}
-        for m in range(2):
-            for i in range(3):
-                for g in range(PASSES):
-                    weave(i, m, g, (i, m, g) in on_vector)
-                for g in range(PASSES):
-                    quant(i, m, g)
-                    multiply(i, m, g)
-                fold(i, m)
+        load_x(0, 0, 1)
+        nc.sync.dma_start(offsets[:], offs)
+        load_x(0, 1, 2)
+        load_x(0, 2, 3)
+        load_x(0, 3, 4)
+        load_x(1, 0, 1)
+        load_x(1, 1, 2)
+        load_x(1, 2, 3)
+        load_x(1, 3, 4)
+        load_w(0, 0)
+        load_w(0, 1)
+        load_w(1, 0)
+        load_w(1, 1)
+        load_w(2, 0)
+        load_w_half(2, 1, 0)
+        load_w_half(2, 1, 1)
+        gather_dense(0)
+        gather_dense(1)
+        gather_dense(2)
+        gather_dense(3)
+        weave_dense()
+        gather(1, 0)
+        quant_x(0)
+        gather(1, 1)
+        gather(1, 2)
+        gather(1, 3)
+        weave(0, 0, 0, False)
+        weave(0, 0, 1, False)
+        quant_x(1)
+        quant(0, 0, 0)
+        quant(0, 0, 1)
+        multiply(0, 0, 0)
+        multiply(0, 0, 1)
+        weave(0, 1, 0, False)
+        weave(0, 1, 1, True)
+        quant(0, 1, 1)
+        quant(0, 1, 0)
+        multiply(0, 1, 1)
+        multiply(0, 1, 0)
+        weave(1, 0, 1, True)
+        weave(1, 0, 0, True)
+        quant(1, 0, 1)
+        quant(1, 0, 0)
+        multiply(1, 0, 1)
+        multiply(1, 0, 0)
+        fold(0, 1)
+        fold(0, 0)
+        weave(1, 1, 0, True)
+        weave(1, 1, 1, True)
+        quant(1, 1, 0)
+        quant(1, 1, 1)
+        multiply(1, 1, 0)
+        multiply(1, 1, 1)
+        weave(2, 0, 0, True)
+        weave(2, 0, 1, True)
+        quant(2, 0, 0)
+        quant(2, 0, 1)
+        multiply(2, 0, 0)
+        multiply(2, 0, 1)
+        weave(2, 1, 0, False)
+        weave(2, 1, 1, False)
+        fold(1, 0)
+        quant(2, 1, 0)
+        multiply(2, 1, 0)
+        fold(1, 1)
+        quant(2, 1, 1)
+        multiply(2, 1, 1)
+        fold(2, 0)
+        fold(2, 1)

@@ -26,7 +26,7 @@ def tile_picked_maxout_max_e_kernel(tc, xT, w1, w2, w3, offs, out):
         keep = ctx.enter_context(tc.tile_pool(name="keep", bufs=1))
         psum = ctx.enter_context(tc.psum_pool(name="psum", bufs=1))
 
-        reuse = {"best_1_1_0":"wraw_2_1_0","best_1_0_0":"wg_2_0_0","best_2_0_256":"wg_2_1_1","x_codes_0":"x_1_0"}
+        reuse = {"x_codes_0":"x_1_0","wc_011":"raw_01","wc_101":"raw_10","best_00":"wg_100","best_01":"wg_101","best_10":"wg_200","best_11":"raw_210","best_20_256":"wg_211"}
 
         def new_tile(shape, dtype, name):
             return keep.tile(shape, dtype, name=name, tag=reuse.get(name, name), align_bytes=64)
@@ -42,14 +42,14 @@ def tile_picked_maxout_max_e_kernel(tc, xT, w1, w2, w3, offs, out):
             for j in range(j0, j1):
                 planes[g, j] = rows[:, (j - j0) * T : (j - j0 + 1) * T]
 
-        def load_w(i, g):
-            rows = new_tile([P, PACK, N], F32, f"wraw_{i}_{g}")
+        def load_w_rows(i, g):
+            rows = new_tile([P, PACK, N], F32, f"raw_{i}{g}")
             nc.sync.dma_start(out=rows[:], in_=ws[i][g * KP : (g + 1) * KP, :].rearrange("(p j) n -> p j n", j=PACK))
             for m in range(2):
                 raw[i, g, m] = rows[:, :, m * P : (m + 1) * P]
 
-        def load_w_half(i, g, m):
-            rows = new_tile([P, PACK, P], F32, f"wraw_{i}_{g}_{m}")
+        def load_w(i, g, m):
+            rows = new_tile([P, PACK, P], F32, f"raw_{i}{g}{m}")
             nc.sync.dma_start(
                 out=rows[:], in_=ws[i][g * KP : (g + 1) * KP, m * P : (m + 1) * P].rearrange("(p j) n -> p j n", j=PACK)
             )
@@ -83,7 +83,7 @@ def tile_picked_maxout_max_e_kernel(tc, xT, w1, w2, w3, offs, out):
             )
 
         def weave(i, g, m, on_vector):
-            grouped[i, g, m] = new_tile([P, P, PACK], BF16, f"wg_{i}_{g}_{m}")
+            grouped[i, g, m] = new_tile([P, P, PACK], BF16, f"wg_{i}{g}{m}")
             dst = grouped[i, g, m][:].rearrange("p (c u) j -> p c j u", u=4)
             src = raw[i, g, m].rearrange("p j (c u) -> p c j u", u=4)
             if on_vector:
@@ -92,8 +92,8 @@ def tile_picked_maxout_max_e_kernel(tc, xT, w1, w2, w3, offs, out):
                 nc.scalar.copy(out=dst, in_=src)
 
         def quant(i, g, m):
-            w_codes[i, g, m] = new_tile([P, P], U32, f"wc_{i}_{g}_{m}")
-            w_scales[i, g, m] = new_tile([P, P], U8, f"wsc_{i}_{g}_{m}")
+            w_codes[i, g, m] = new_tile([P, P], U32, f"wc_{i}{g}{m}")
+            w_scales[i, g, m] = new_tile([P, P], U8, f"wsc_{i}{g}{m}")
             nc.vector.quantize_mx(
                 out=w_codes[i, g, m][:].bitcast(FP8X4),
                 scales=w_scales[i, g, m][:],
@@ -101,12 +101,12 @@ def tile_picked_maxout_max_e_kernel(tc, xT, w1, w2, w3, offs, out):
             )
 
         def spans(i, m):
-            return [(0, S // 2), (S // 2, S)] if i == 2 else [(0, S)]
+            return [(0, 256), (256, 512)] if i == 2 else [(0, S)]
 
         def multiply(i, g, m):
             for a, b in spans(i, m):
                 if g == 0:
-                    acc[i, m, a] = psum.tile([P, b - a], F32, name=f"acc_{i}_{m}_{a}")
+                    acc[i, m, a] = psum.tile([P, b - a], F32, name=f"acc_{i}{m}_{a}")
                 nc.tensor.matmul_mx(
                     out=acc[i, m, a][:],
                     lhsT=w_codes[i, g, m][:].bitcast(FP8X4),
@@ -117,83 +117,62 @@ def tile_picked_maxout_max_e_kernel(tc, xT, w1, w2, w3, offs, out):
                     stop=(g == PASSES - 1),
                 )
 
-        def fold(i, m):
-            for a, b in spans(i, m):
-                new = new_tile([P, b - a], F32, f"best_{i}_{m}_{a}")
-                if i == 0:
-                    nc.scalar.copy(out=new[:], in_=acc[i, m, a][:])
-                else:
-                    nc.vector.tensor_tensor(out=new[:], in0=acc[i, m, a][:], in1=best[i - 1, m][:, a:b], op=MAX)
-                if i == 2:
-                    nc.sync.dma_start(out=out[m * P : (m + 1) * P, a:b], in_=new[:])
-                else:
-                    best[i, m] = new
+        def fold_spans(i, m):
+            return spans(i, m)
 
-        load_x(0, 0, 1)
+        def fold(i, m):
+            if i < 2:
+                best[i, m] = new_tile([P, S], F32, f"best_{i}{m}")
+            for a, b in fold_spans(i, m):
+                start = max(s0 for s0, s1 in spans(i, m) if s0 <= a)
+                sums = acc[i, m, start][:, a - start : b - start]
+                if i == 0:
+                    nc.scalar.copy(out=best[i, m][:, a:b], in_=sums)
+                elif i == 1:
+                    nc.vector.tensor_tensor(out=best[i, m][:, a:b], in0=sums, in1=best[0, m][:, a:b], op=MAX)
+                else:
+                    result = new_tile([P, b - a], F32, f"best_{i}{m}_{a}")
+                    nc.vector.tensor_tensor(out=result[:], in0=sums, in1=best[1, m][:, a:b], op=MAX)
+                    nc.sync.dma_start(out=out[m * P : (m + 1) * P, a:b], in_=result[:])
+
+        load_x(0, 0, 2)
         nc.sync.dma_start(offsets[:], offs)
-        load_x(0, 1, 2)
-        load_x(0, 2, 3)
-        load_x(0, 3, 4)
-        load_x(1, 0, 1)
-        load_x(1, 1, 2)
-        load_x(1, 2, 3)
-        load_x(1, 3, 4)
-        load_w(0, 0)
-        load_w(0, 1)
-        load_w(1, 0)
-        load_w(1, 1)
-        load_w(2, 0)
-        load_w_half(2, 1, 0)
-        load_w_half(2, 1, 1)
-        gather_dense(0)
-        gather_dense(1)
-        gather_dense(2)
-        gather_dense(3)
+        load_x(0, 2, 4)
+        for j in range(PACK):
+            load_x(1, j, j + 1)
+        for i, g in ((0, 0), (0, 1), (1, 0), (1, 1), (2, 0)):
+            load_w_rows(i, g)
+        load_w(2, 1, 0)
+        load_w(2, 1, 1)
+        for j in range(PACK):
+            gather_dense(j)
         weave_dense()
         gather(1, 0)
         quant_x(0)
-        gather(1, 1)
-        gather(1, 2)
-        gather(1, 3)
-        weave(0, 0, 0, False)
-        weave(0, 0, 1, False)
+        for j in range(1, PACK):
+            gather(1, j)
         quant_x(1)
-        quant(0, 0, 0)
-        quant(0, 0, 1)
-        multiply(0, 0, 0)
-        multiply(0, 0, 1)
-        weave(0, 1, 0, False)
-        weave(0, 1, 1, True)
-        quant(0, 1, 1)
-        quant(0, 1, 0)
-        multiply(0, 1, 1)
-        multiply(0, 1, 0)
-        weave(1, 0, 1, True)
-        weave(1, 0, 0, True)
-        quant(1, 0, 1)
-        quant(1, 0, 0)
-        multiply(1, 0, 1)
-        multiply(1, 0, 0)
-        fold(0, 1)
+        def rows(i, g, on_vector):
+            for m in range(2):
+                weave(i, g, m, on_vector[m])
+            for m in range(2):
+                quant(i, g, m)
+            for m in range(2):
+                multiply(i, g, m)
+
+        rows(0, 0, (False, False))
+        rows(0, 1, (False, True))
+        rows(1, 0, (False, True))
         fold(0, 0)
-        weave(1, 1, 0, True)
-        weave(1, 1, 1, True)
-        quant(1, 1, 0)
-        quant(1, 1, 1)
-        multiply(1, 1, 0)
-        multiply(1, 1, 1)
-        weave(2, 0, 0, True)
-        weave(2, 0, 1, True)
-        quant(2, 0, 0)
-        quant(2, 0, 1)
-        multiply(2, 0, 0)
-        multiply(2, 0, 1)
-        weave(2, 1, 0, False)
-        weave(2, 1, 1, False)
+        fold(0, 1)
+        rows(1, 1, (True, True))
+        rows(2, 0, (True, True))
         fold(1, 0)
+        weave(2, 1, 0, False)
         quant(2, 1, 0)
         multiply(2, 1, 0)
         fold(1, 1)
+        weave(2, 1, 1, False)
         quant(2, 1, 1)
         multiply(2, 1, 1)
         fold(2, 0)

@@ -71,8 +71,8 @@ def tile_picked_maxout_max_e_kernel(tc, xT, w1, w2, w3, offs, out):
         def weave_dense():
             picked[0] = new_tile([P, S, PACK], BF16, "picked_0")
             nc.scalar.copy(
-                out=picked[0][:].rearrange("p (c u) j -> p c j u", u=4),
-                in_=dense[:].rearrange("p j (c u) -> p c j u", u=4),
+                out=picked[0][:].rearrange("p (c u) j -> p c j u", u=2),
+                in_=dense[:].rearrange("p j (c u) -> p c j u", u=2),
             )
 
         def quant_x(g):
@@ -84,8 +84,8 @@ def tile_picked_maxout_max_e_kernel(tc, xT, w1, w2, w3, offs, out):
 
         def weave(i, g, m, on_vector):
             grouped[i, g, m] = new_tile([P, P, PACK], BF16, f"wg_{i}{g}{m}")
-            dst = grouped[i, g, m][:].rearrange("p (c u) j -> p c j u", u=4)
-            src = raw[i, g, m].rearrange("p j (c u) -> p c j u", u=4)
+            dst = grouped[i, g, m][:].rearrange("p (c u) j -> p c j u", u=2)
+            src = raw[i, g, m].rearrange("p j (c u) -> p c j u", u=2)
             if on_vector:
                 nc.vector.tensor_copy(out=dst, in_=src)
             else:

@@ -36,9 +36,9 @@ def tile_picked_maxout_max_e_kernel(tc, xT, w1, w2, w3, offs, out):
         planes = {}
         raw = {}
 
-        def load_x(g, j0, j1):
+        def load_x(g, j0, j1, queue=nc.sync):
             rows = new_tile([P, (j1 - j0) * T], F32, f"x_{g}_{j0}")
-            nc.sync.dma_start(out=rows[:], in_=x_rows[g][:, j0:j1, :].rearrange("p j t -> p (j t)"))
+            queue.dma_start(out=rows[:], in_=x_rows[g][:, j0:j1, :].rearrange("p j t -> p (j t)"))
             for j in range(j0, j1):
                 planes[g, j] = rows[:, (j - j0) * T : (j - j0 + 1) * T]
 
@@ -135,9 +135,11 @@ def tile_picked_maxout_max_e_kernel(tc, xT, w1, w2, w3, offs, out):
                     nc.vector.tensor_tensor(out=result[:], in0=sums, in1=best[1, m][:, a:b], op=MAX)
                     nc.sync.dma_start(out=out[m * P : (m + 1) * P, a:b], in_=result[:])
 
-        load_x(0, 0, 2)
+        load_x(0, 0, 1, nc.scalar)
         nc.sync.dma_start(offsets[:], offs)
-        load_x(0, 2, 4)
+        load_x(0, 1, 2)
+        load_x(0, 2, 3, nc.scalar)
+        load_x(0, 3, 4)
         for j in range(PACK):
             load_x(1, j, j + 1)
         for i, g in ((0, 0), (0, 1), (1, 0), (1, 1), (2, 0)):

@@ -12,11 +12,14 @@ U16 = mybir.dt.uint16
 U8 = mybir.dt.uint8
 FP8X4 = mybir.dt.float8_e4m3fn_x4
 MAX = mybir.AluOpType.max
+MULT = mybir.AluOpType.mult
+ADD = mybir.AluOpType.add
 
 P = 128
 PACK = 4
 KP = P * PACK
 PASSES = K // KP
+HALF = S // 2
 
 
 def tile_picked_maxout_max_e_kernel(tc, xT, w1, w2, w3, offs, out):
@@ -26,47 +29,30 @@ def tile_picked_maxout_max_e_kernel(tc, xT, w1, w2, w3, offs, out):
         keep = ctx.enter_context(tc.tile_pool(name="keep", bufs=1))
         psum = ctx.enter_context(tc.psum_pool(name="psum", bufs=1))
 
-        reuse = {"x_codes_0":"x_1_0","wc_011":"raw_01","wc_101":"raw_10","best_00":"wg_100","best_01":"wg_101","best_10":"wg_200","best_11":"raw_210","best_20_256":"wg_211"}
-
-        def new_tile(shape, dtype, name):
-            return keep.tile(shape, dtype, name=name, tag=reuse.get(name, name), align_bytes=64)
+        def new_tile(shape, dtype, name, slot=None):
+            return keep.tile(shape, dtype, name=name, tag=slot or name, align_bytes=64)
 
         offsets = keep.tile([P, S // 16], U16, name="offsets")
         x_rows = xT.rearrange("(g p j) t -> g p j t", p=P, j=PACK)
-        planes = {}
-        raw = {}
+        planes, raw = {}, {}
 
-        def load_x(g, j0, j1, queue=nc.sync):
-            rows = new_tile([P, (j1 - j0) * T], F32, f"x_{g}_{j0}")
-            queue.dma_start(out=rows[:], in_=x_rows[g][:, j0:j1, :].rearrange("p j t -> p (j t)"))
-            for j in range(j0, j1):
-                planes[g, j] = rows[:, (j - j0) * T : (j - j0 + 1) * T]
+        def load_x(g, j, queue=nc.sync):
+            planes[g, j] = new_tile([P, T], F32, f"x_{g}{j}")
+            queue.dma_start(out=planes[g, j][:], in_=x_rows[g][:, j, :])
 
-        def load_w_rows(i, g):
-            rows = new_tile([P, PACK, N], F32, f"raw_{i}{g}")
-            nc.sync.dma_start(out=rows[:], in_=ws[i][g * KP : (g + 1) * KP, :].rearrange("(p j) n -> p j n", j=PACK))
-            for m in range(2):
-                raw[i, g, m] = rows[:, :, m * P : (m + 1) * P]
-
-        def load_w(i, g, m):
-            rows = new_tile([P, PACK, P], F32, f"raw_{i}{g}{m}")
-            nc.sync.dma_start(
-                out=rows[:], in_=ws[i][g * KP : (g + 1) * KP, m * P : (m + 1) * P].rearrange("(p j) n -> p j n", j=PACK)
-            )
-            raw[i, g, m] = rows[:]
+        def load_w(i, g, tiles, queue=nc.sync):
+            cols = slice(tiles[0] * P, (tiles[-1] + 1) * P)
+            rows = new_tile([P, PACK, P * len(tiles)], F32, f"raw_{i}{g}{tiles[0]}")
+            queue.dma_start(out=rows[:], in_=ws[i][g * KP : (g + 1) * KP, cols].rearrange("(p j) n -> p j n", j=PACK))
+            for m in tiles:
+                raw[i, g, m] = rows[:, :, (m - tiles[0]) * P : (m - tiles[0] + 1) * P]
 
         picked, x_codes, x_scales = {}, {}, {}
-        grouped, w_codes, w_scales, acc, best = {}, {}, {}, {}, {}
-
-        def gather(g, j):
-            if j == 0:
-                picked[g] = new_tile([P, S, PACK], BF16, f"picked_{g}")
-            nc.vector.tensor_copy(out=picked[g][:, :, j], in_=planes[g, j].indirect(offsets[:]))
-
+        woven, w_codes, w_scales, acc, best = {}, {}, {}, {}, {}
         dense = new_tile([P, PACK, S], F32, "dense")
 
         def gather_dense(j):
-            nc.vector.tensor_copy(out=dense[:, j, :], in_=planes[0, j].indirect(offsets[:]))
+            nc.vector.tensor_copy(out=dense[:, j, :], in_=planes[0, j][:].indirect(offsets[:]))
 
         def weave_dense():
             picked[0] = new_tile([P, S, PACK], BF16, "picked_0")
@@ -75,36 +61,39 @@ def tile_picked_maxout_max_e_kernel(tc, xT, w1, w2, w3, offs, out):
                 in_=dense[:].rearrange("p j (c u) -> p c j u", u=2),
             )
 
-        def quant_x(g):
-            x_codes[g] = new_tile([P, S], U32, f"x_codes_{g}")
+        def gather_woven(j):
+            if j == 0:
+                picked[1] = new_tile([P, S, PACK], BF16, "picked_1")
+            nc.vector.tensor_copy(out=picked[1][:, :, j], in_=planes[1, j][:].indirect(offsets[:]))
+
+        def quant_x(g, slot=None):
+            x_codes[g] = new_tile([P, S], U32, f"x_codes_{g}", slot)
             x_scales[g] = new_tile([P, S], U8, f"x_scales_{g}")
             nc.vector.quantize_mx(
                 out=x_codes[g][:].bitcast(FP8X4), scales=x_scales[g][:], in_=picked[g][:].rearrange("p s j -> p (s j)")
             )
 
-        def weave(i, g, m, on_vector):
-            grouped[i, g, m] = new_tile([P, P, PACK], BF16, f"wg_{i}{g}{m}")
-            dst = grouped[i, g, m][:].rearrange("p (c u) j -> p c j u", u=2)
-            src = raw[i, g, m].rearrange("p j (c u) -> p c j u", u=2)
-            if on_vector:
+        def weave(i, g, m, engine, a=0, b=P, slot=None):
+            if (i, g, m) not in woven:
+                woven[i, g, m] = new_tile([P, P * PACK], BF16, f"woven_{i}{g}{m}", slot)
+            dst = woven[i, g, m][:, a * PACK : b * PACK].rearrange("p (c u j) -> p c j u", u=2, j=PACK)
+            src = raw[i, g, m][:, :, a:b].rearrange("p j (c u) -> p c j u", u=2)
+            if engine == "vector":
                 nc.vector.tensor_copy(out=dst, in_=src)
-            else:
+            elif engine == "scalar":
                 nc.scalar.copy(out=dst, in_=src)
+            else:
+                nc.gpsimd.tensor_scalar(out=dst, in0=src, scalar1=1.0, scalar2=0.0, op0=MULT, op1=ADD)
 
-        def quant(i, g, m):
-            w_codes[i, g, m] = new_tile([P, P], U32, f"wc_{i}{g}{m}")
-            w_scales[i, g, m] = new_tile([P, P], U8, f"wsc_{i}{g}{m}")
+        def quant(i, g, m, slot=None):
+            w_codes[i, g, m] = new_tile([P, P], U32, f"codes_{i}{g}{m}", slot)
+            w_scales[i, g, m] = new_tile([P, P], U8, f"scales_{i}{g}{m}")
             nc.vector.quantize_mx(
-                out=w_codes[i, g, m][:].bitcast(FP8X4),
-                scales=w_scales[i, g, m][:],
-                in_=grouped[i, g, m][:].rearrange("p n j -> p (n j)"),
+                out=w_codes[i, g, m][:].bitcast(FP8X4), scales=w_scales[i, g, m][:], in_=woven[i, g, m][:]
             )
 
-        def spans(i, m):
-            return [(0, 256), (256, 512)] if i == 2 else [(0, S)]
-
-        def multiply(i, g, m):
-            for a, b in spans(i, m):
+        def multiply(i, g, m, spans=((0, S),)):
+            for a, b in spans:
                 if g == 0:
                     acc[i, m, a] = psum.tile([P, b - a], F32, name=f"acc_{i}{m}_{a}")
                 nc.tensor.matmul_mx(
@@ -117,65 +106,71 @@ def tile_picked_maxout_max_e_kernel(tc, xT, w1, w2, w3, offs, out):
                     stop=(g == PASSES - 1),
                 )
 
-        def fold_spans(i, m):
-            return spans(i, m)
+        def part(tiles, i, m, a, b):
+            start = max(s for (ii, mm, s) in tiles if (ii, mm) == (i, m) and s <= a)
+            return tiles[i, m, start][:, a - start : b - start]
 
-        def fold(i, m):
-            if i < 2:
-                best[i, m] = new_tile([P, S], F32, f"best_{i}{m}")
-            for a, b in fold_spans(i, m):
-                start = max(s0 for s0, s1 in spans(i, m) if s0 <= a)
-                sums = acc[i, m, start][:, a - start : b - start]
-                if i == 0:
-                    nc.scalar.copy(out=best[i, m][:, a:b], in_=sums)
-                elif i == 1:
-                    nc.vector.tensor_tensor(out=best[i, m][:, a:b], in0=sums, in1=best[0, m][:, a:b], op=MAX)
-                else:
-                    result = new_tile([P, b - a], F32, f"best_{i}{m}_{a}")
-                    nc.vector.tensor_tensor(out=result[:], in0=sums, in1=best[1, m][:, a:b], op=MAX)
-                    nc.sync.dma_start(out=out[m * P : (m + 1) * P, a:b], in_=result[:])
+        def fold(i, m, a=0, b=S, slot=None, queue=nc.sync):
+            best[i, m, a] = new_tile([P, b - a], F32, f"best_{i}{m}_{a}", slot)
+            sums = part(acc, i, m, a, b)
+            if i == 0:
+                nc.scalar.copy(out=best[i, m, a][:], in_=sums)
+            else:
+                nc.vector.tensor_tensor(out=best[i, m, a][:], in0=sums, in1=part(best, i - 1, m, a, b), op=MAX)
+            if i == 2:
+                queue.dma_start(out=out[m * P : (m + 1) * P, a:b], in_=best[i, m, a][:])
 
-        load_x(0, 0, 1, nc.scalar)
+        probes = []
+
+        def probe(ap):
+            probes.append(new_tile([P, 1], ap.dtype, f"probe_{len(probes)}"))
+            nc.gpsimd.tensor_copy(out=probes[-1][:], in_=ap)
+
+        load_x(0, 0, nc.scalar)
+        load_x(0, 1)
         nc.sync.dma_start(offsets[:], offs)
-        load_x(0, 1, 2)
-        load_x(0, 2, 3, nc.scalar)
-        load_x(0, 3, 4)
+        load_x(0, 2, nc.scalar)
+        load_x(0, 3)
         for j in range(PACK):
-            load_x(1, j, j + 1)
+            load_x(1, j)
         for i, g in ((0, 0), (0, 1), (1, 0), (1, 1), (2, 0)):
-            load_w_rows(i, g)
-        load_w(2, 1, 0)
-        load_w(2, 1, 1)
+            load_w(i, g, (0, 1))
+        load_w(2, 1, (0,))
+        load_w(2, 1, (1,))
         for j in range(PACK):
             gather_dense(j)
         weave_dense()
-        gather(1, 0)
-        quant_x(0)
+        gather_woven(0)
+        quant_x(0, slot="x_10")
         for j in range(1, PACK):
-            gather(1, j)
+            gather_woven(j)
         quant_x(1)
-        def rows(i, g, on_vector):
+        halves = ((0, HALF), (HALF, S))
+        def rows(i, g, engines, slots=(None, None)):
+            spans = halves if i == 2 else ((0, S),)
             for m in range(2):
-                weave(i, g, m, on_vector[m])
+                weave(i, g, m, engines[m])
             for m in range(2):
-                quant(i, g, m)
+                quant(i, g, m, slot=slots[m])
             for m in range(2):
-                multiply(i, g, m)
+                multiply(i, g, m, spans)
 
-        rows(0, 0, (False, False))
-        rows(0, 1, (False, True))
-        rows(1, 0, (False, True))
-        fold(0, 0)
-        fold(0, 1)
-        rows(1, 1, (True, True))
-        rows(2, 0, (True, True))
-        fold(1, 0)
-        weave(2, 1, 0, False)
+        rows(0, 0, ("scalar", "scalar"))
+        rows(0, 1, ("scalar", "vector"), (None, "raw_010"))
+        rows(1, 0, ("scalar", "vector"), (None, "raw_100"))
+        fold(0, 0, slot="woven_100")
+        fold(0, 1, slot="woven_101")
+        rows(1, 1, ("vector", "vector"))
+        rows(2, 0, ("vector", "vector"))
+        fold(1, 0, slot="woven_200")
+        weave(2, 1, 0, "scalar")
         quant(2, 1, 0)
-        multiply(2, 1, 0)
-        fold(1, 1)
-        weave(2, 1, 1, False)
+        multiply(2, 1, 0, halves)
+        fold(1, 1, slot="raw_210")
+        weave(2, 1, 1, "scalar")
         quant(2, 1, 1)
-        multiply(2, 1, 1)
-        fold(2, 0)
-        fold(2, 1)
+        multiply(2, 1, 1, halves)
+        fold(2, 0, 0, HALF)
+        fold(2, 0, HALF, S, slot="woven_211")
+        fold(2, 1, 0, HALF)
+        fold(2, 1, HALF, S)

@@ -66,6 +66,22 @@ def tile_picked_maxout_max_e_kernel(tc, xT, w1, w2, w3, offs, out):
                 picked[1] = new_tile([P, S, PACK], BF16, "picked_1")
             nc.vector.tensor_copy(out=picked[1][:, :, j], in_=planes[1, j][:].indirect(offsets[:]))
 
+        def last_plane_in_halves():
+            x_codes[1] = new_tile([P, S], U32, "x_codes_1")
+            x_scales[1] = new_tile([P, S], U8, "x_scales_1")
+            flat = picked[1][:].rearrange("p s j -> p (s j)")
+            for a in (0, HALF):
+                nc.vector.tensor_copy(
+                    out=picked[1][:, a : a + HALF, PACK - 1],
+                    in_=planes[1, PACK - 1][:].indirect(offsets[:, a // 16 : (a + HALF) // 16]),
+                )
+            for a in (0, HALF):
+                nc.vector.quantize_mx(
+                    out=x_codes[1][:, a : a + HALF].bitcast(FP8X4),
+                    scales=x_scales[1][:, a : a + HALF],
+                    in_=flat[:, a * PACK : (a + HALF) * PACK],
+                )
+
         def quant_x(g, slot=None):
             x_codes[g] = new_tile([P, S], U32, f"x_codes_{g}", slot)
             x_scales[g] = new_tile([P, S], U8, f"x_scales_{g}")
@@ -92,9 +108,9 @@ def tile_picked_maxout_max_e_kernel(tc, xT, w1, w2, w3, offs, out):
                 out=w_codes[i, g, m][:].bitcast(FP8X4), scales=w_scales[i, g, m][:], in_=woven[i, g, m][:]
             )
 
-        def multiply(i, g, m, spans=((0, S),)):
+        def multiply(i, g, m, spans=((0, S),), first=0):
             for a, b in spans:
-                if g == 0:
+                if g == first:
                     acc[i, m, a] = psum.tile([P, b - a], F32, name=f"acc_{i}{m}_{a}")
                 nc.tensor.matmul_mx(
                     out=acc[i, m, a][:],
@@ -102,8 +118,8 @@ def tile_picked_maxout_max_e_kernel(tc, xT, w1, w2, w3, offs, out):
                     lhsT_scale=w_scales[i, g, m][:],
                     rhs=x_codes[g][:, a:b].bitcast(FP8X4),
                     rhs_scale=x_scales[g][:, a:b],
-                    start=(g == 0),
-                    stop=(g == PASSES - 1),
+                    start=(g == first),
+                    stop=(g != first),
                 )
 
         def part(tiles, i, m, a, b):
@@ -142,25 +158,28 @@ def tile_picked_maxout_max_e_kernel(tc, xT, w1, w2, w3, offs, out):
         weave_dense()
         gather_woven(0)
         quant_x(0, slot="x_10")
-        for j in range(1, PACK):
+        for j in range(1, PACK - 1):
             gather_woven(j)
-        quant_x(1)
+        last_plane_in_halves()
         halves = ((0, HALF), (HALF, S))
-        def rows(i, g, engines, slots=(None, None)):
+        def rows(i, g, engines, order=(0, 1), slots=(None, None)):
             spans = halves if i == 2 else ((0, S),)
-            for m in range(2):
+            for m in order:
                 weave(i, g, m, engines[m])
-            for m in range(2):
+            for m in order:
                 quant(i, g, m, slot=slots[m])
-            for m in range(2):
-                multiply(i, g, m, spans)
+            for m in order:
+                if (i, m) != (1, 1):
+                    multiply(i, g, m, spans)
 
         rows(0, 0, ("scalar", "scalar"))
-        rows(0, 1, ("scalar", "vector"), (None, "raw_010"))
-        rows(1, 0, ("scalar", "vector"), (None, "raw_100"))
+        rows(0, 1, ("vector", "scalar"))
+        rows(1, 0, ("scalar", "vector"), (1, 0))
         fold(0, 0, slot="woven_100")
         fold(0, 1, slot="woven_101")
         rows(1, 1, ("vector", "vector"))
+        multiply(1, 1, 1, first=1)
+        multiply(1, 0, 1, first=1)
         rows(2, 0, ("vector", "vector"))
         fold(1, 0, slot="woven_200")
         weave(2, 1, 0, "scalar")

@@ -30,7 +30,7 @@ def tile_picked_maxout_max_e_kernel(tc, xT, w1, w2, w3, offs, out):
         psum = ctx.enter_context(tc.psum_pool(name="psum", bufs=1))
 
         def new_tile(shape, dtype, name, slot=None):
-            return keep.tile(shape, dtype, name=name, tag=slot or name, align_bytes=64)
+            return keep.tile(shape, dtype, name=name, tag=slot or name, align_bytes=256)
 
         offsets = keep.tile([P, S // 16], U16, name="offsets")
         x_rows = xT.rearrange("(g p j) t -> g p j t", p=P, j=PACK)

@@ -12,14 +12,16 @@ U16 = mybir.dt.uint16
 U8 = mybir.dt.uint8
 FP8X4 = mybir.dt.float8_e4m3fn_x4
 MAX = mybir.AluOpType.max
-MULT = mybir.AluOpType.mult
-ADD = mybir.AluOpType.add
 
 P = 128
 PACK = 4
 KP = P * PACK
-PASSES = K // KP
 HALF = S // 2
+GROUP = 16
+PAIR = 2
+ALIGN = 256
+WHOLE = ((0, S),)
+HALVES = ((0, HALF), (HALF, S))
 
 
 def tile_picked_maxout_max_e_kernel(tc, xT, w1, w2, w3, offs, out):
@@ -30,85 +32,65 @@ def tile_picked_maxout_max_e_kernel(tc, xT, w1, w2, w3, offs, out):
         psum = ctx.enter_context(tc.psum_pool(name="psum", bufs=1))
 
         def new_tile(shape, dtype, name, slot=None):
-            return keep.tile(shape, dtype, name=name, tag=slot or name, align_bytes=256)
+            return keep.tile(shape, dtype, name=name, tag=slot or name, align_bytes=ALIGN)
 
-        offsets = keep.tile([P, S // 16], U16, name="offsets")
+        offsets = keep.tile([P, S // GROUP], U16, name="offsets")
         x_rows = xT.rearrange("(g p j) t -> g p j t", p=P, j=PACK)
         planes, raw = {}, {}
 
-        def load_x(g, j, queue=nc.sync):
+        def load_plane(g, j, queue=nc.sync):
             planes[g, j] = new_tile([P, T], F32, f"x_{g}{j}")
             queue.dma_start(out=planes[g, j][:], in_=x_rows[g][:, j, :])
 
-        def load_w(i, g, tiles, queue=nc.sync):
+        def load_weights(i, g, tiles):
             cols = slice(tiles[0] * P, (tiles[-1] + 1) * P)
             rows = new_tile([P, PACK, P * len(tiles)], F32, f"raw_{i}{g}{tiles[0]}")
-            queue.dma_start(out=rows[:], in_=ws[i][g * KP : (g + 1) * KP, cols].rearrange("(p j) n -> p j n", j=PACK))
+            nc.sync.dma_start(
+                out=rows[:], in_=ws[i][g * KP : (g + 1) * KP, cols].rearrange("(p j) n -> p j n", j=PACK)
+            )
             for m in tiles:
                 raw[i, g, m] = rows[:, :, (m - tiles[0]) * P : (m - tiles[0] + 1) * P]
 
         picked, x_codes, x_scales = {}, {}, {}
         woven, w_codes, w_scales, acc, best = {}, {}, {}, {}, {}
-        dense = new_tile([P, PACK, S], F32, "dense")
+        dense = {a: new_tile([P, PACK, HALF], F32, f"dense_{a}") for a, b in HALVES}
 
-        def gather_dense(j):
-            nc.vector.tensor_copy(out=dense[:, j, :], in_=planes[0, j][:].indirect(offsets[:]))
-
-        def weave_dense():
-            picked[0] = new_tile([P, S, PACK], BF16, "picked_0")
-            nc.scalar.copy(
-                out=picked[0][:].rearrange("p (c u) j -> p c j u", u=2),
-                in_=dense[:].rearrange("p j (c u) -> p c j u", u=2),
+        def gather_dense(j, a, b):
+            nc.vector.tensor_copy(
+                out=dense[a][:, j, :], in_=planes[0, j][:].indirect(offsets[:, a // GROUP : b // GROUP])
             )
 
-        def gather_woven(j):
-            if j == 0:
-                picked[1] = new_tile([P, S, PACK], BF16, "picked_1")
-            nc.vector.tensor_copy(out=picked[1][:, :, j], in_=planes[1, j][:].indirect(offsets[:]))
+        def gather_woven(j, a=0, b=S):
+            nc.vector.tensor_copy(
+                out=picked[1][:, a:b, j], in_=planes[1, j][:].indirect(offsets[:, a // GROUP : b // GROUP])
+            )
 
-        def last_plane_in_halves():
-            x_codes[1] = new_tile([P, S], U32, "x_codes_1")
-            x_scales[1] = new_tile([P, S], U8, "x_scales_1")
-            flat = picked[1][:].rearrange("p s j -> p (s j)")
-            for a in (0, HALF):
-                nc.vector.tensor_copy(
-                    out=picked[1][:, a : a + HALF, PACK - 1],
-                    in_=planes[1, PACK - 1][:].indirect(offsets[:, a // 16 : (a + HALF) // 16]),
-                )
-            for a in (0, HALF):
-                nc.vector.quantize_mx(
-                    out=x_codes[1][:, a : a + HALF].bitcast(FP8X4),
-                    scales=x_scales[1][:, a : a + HALF],
-                    in_=flat[:, a * PACK : (a + HALF) * PACK],
-                )
-
-        def quant_x(g, slot=None):
+        def token_tiles(g, slot=None):
             x_codes[g] = new_tile([P, S], U32, f"x_codes_{g}", slot)
             x_scales[g] = new_tile([P, S], U8, f"x_scales_{g}")
+
+        def quantise_tokens(g, a=0, b=S):
             nc.vector.quantize_mx(
-                out=x_codes[g][:].bitcast(FP8X4), scales=x_scales[g][:], in_=picked[g][:].rearrange("p s j -> p (s j)")
+                out=x_codes[g][:, a:b].bitcast(FP8X4),
+                scales=x_scales[g][:, a:b],
+                in_=picked[g][:].rearrange("p s j -> p (s j)")[:, a * PACK : b * PACK],
             )
 
-        def weave(i, g, m, engine, a=0, b=P, slot=None):
-            if (i, g, m) not in woven:
-                woven[i, g, m] = new_tile([P, P * PACK], BF16, f"woven_{i}{g}{m}", slot)
-            dst = woven[i, g, m][:, a * PACK : b * PACK].rearrange("p (c u j) -> p c j u", u=2, j=PACK)
-            src = raw[i, g, m][:, :, a:b].rearrange("p j (c u) -> p c j u", u=2)
-            if engine == "vector":
-                nc.vector.tensor_copy(out=dst, in_=src)
-            elif engine == "scalar":
-                nc.scalar.copy(out=dst, in_=src)
-            else:
-                nc.gpsimd.tensor_scalar(out=dst, in0=src, scalar1=1.0, scalar2=0.0, op0=MULT, op1=ADD)
+        def weave(i, g, m, copy):
+            woven[i, g, m] = new_tile([P, P * PACK], BF16, f"woven_{i}{g}{m}")
+            copy(
+                out=woven[i, g, m][:].rearrange("p (c u j) -> p c j u", u=PAIR, j=PACK),
+                in_=raw[i, g, m].rearrange("p j (c u) -> p c j u", u=PAIR),
+            )
 
-        def quant(i, g, m, slot=None):
-            w_codes[i, g, m] = new_tile([P, P], U32, f"codes_{i}{g}{m}", slot)
+        def quantise_weights(i, g, m):
+            w_codes[i, g, m] = new_tile([P, P], U32, f"codes_{i}{g}{m}")
             w_scales[i, g, m] = new_tile([P, P], U8, f"scales_{i}{g}{m}")
             nc.vector.quantize_mx(
                 out=w_codes[i, g, m][:].bitcast(FP8X4), scales=w_scales[i, g, m][:], in_=woven[i, g, m][:]
             )
 
-        def multiply(i, g, m, spans=((0, S),), first=0):
+        def multiply(i, g, m, spans=WHOLE, first=0):
             for a, b in spans:
                 if g == first:
                     acc[i, m, a] = psum.tile([P, b - a], F32, name=f"acc_{i}{m}_{a}")
@@ -122,74 +104,89 @@ def tile_picked_maxout_max_e_kernel(tc, xT, w1, w2, w3, offs, out):
                     stop=(g != first),
                 )
 
-        def part(tiles, i, m, a, b):
-            start = max(s for (ii, mm, s) in tiles if (ii, mm) == (i, m) and s <= a)
-            return tiles[i, m, start][:, a - start : b - start]
+        def prepare(i, g, copies, order=(0, 1)):
+            for m in order:
+                weave(i, g, m, copies[m])
+            for m in order:
+                quantise_weights(i, g, m)
 
-        def fold(i, m, a=0, b=S, slot=None, queue=nc.sync):
-            best[i, m, a] = new_tile([P, b - a], F32, f"best_{i}{m}_{a}", slot)
-            sums = part(acc, i, m, a, b)
-            if i == 0:
-                nc.scalar.copy(out=best[i, m, a][:], in_=sums)
-            else:
-                nc.vector.tensor_tensor(out=best[i, m, a][:], in0=sums, in1=part(best, i - 1, m, a, b), op=MAX)
-            if i == 2:
-                queue.dma_start(out=out[m * P : (m + 1) * P, a:b], in_=best[i, m, a][:])
+        def keep_first(m, slot):
+            best[0, m] = new_tile([P, S], F32, f"best_0{m}_0", slot)
+            nc.scalar.copy(out=best[0, m][:], in_=acc[0, m, 0][:])
 
-        probes = []
+        def max_second(m, slot):
+            best[1, m] = new_tile([P, S], F32, f"best_1{m}_0", slot)
+            nc.vector.tensor_tensor(out=best[1, m][:], in0=acc[1, m, 0][:], in1=best[0, m][:], op=MAX)
 
-        def probe(ap):
-            probes.append(new_tile([P, 1], ap.dtype, f"probe_{len(probes)}"))
-            nc.gpsimd.tensor_copy(out=probes[-1][:], in_=ap)
+        def max_third_and_store(m, a, b, slot=None):
+            result = new_tile([P, b - a], F32, f"best_2{m}_{a}", slot)
+            nc.vector.tensor_tensor(out=result[:], in0=acc[2, m, a][:], in1=best[1, m][:, a:b], op=MAX)
+            nc.sync.dma_start(out=out[m * P : (m + 1) * P, a:b], in_=result[:])
 
-        load_x(0, 0, nc.scalar)
-        load_x(0, 1)
+        on_vector, on_scalar = nc.vector.tensor_copy, nc.scalar.copy
+
+        load_plane(0, 0, nc.scalar)
+        load_plane(0, 1)
         nc.sync.dma_start(offsets[:], offs)
-        load_x(0, 2, nc.scalar)
-        load_x(0, 3)
+        load_plane(0, 2, nc.scalar)
+        load_plane(0, 3)
         for j in range(PACK):
-            load_x(1, j)
+            load_plane(1, j)
         for i, g in ((0, 0), (0, 1), (1, 0), (1, 1), (2, 0)):
-            load_w(i, g, (0, 1))
-        load_w(2, 1, (0,))
-        load_w(2, 1, (1,))
-        for j in range(PACK):
-            gather_dense(j)
-        weave_dense()
+            load_weights(i, g, (0, 1))
+        load_weights(2, 1, (0,))
+        load_weights(2, 1, (1,))
+
+        for pair in ((0, 1), (2, 3)):
+            for a, b in HALVES:
+                for j in pair:
+                    gather_dense(j, a, b)
+        picked[0] = new_tile([P, S, PACK], BF16, "picked_0")
+        for a, b in HALVES:
+            nc.scalar.copy(
+                out=picked[0][:, a:b, :].rearrange("p (c u) j -> p c j u", u=PAIR),
+                in_=dense[a][:].rearrange("p j (c u) -> p c j u", u=PAIR),
+            )
+        picked[1] = new_tile([P, S, PACK], BF16, "picked_1")
         gather_woven(0)
-        quant_x(0, slot="x_10")
+        token_tiles(0, slot="x_10")
+        quantise_tokens(0)
         for j in range(1, PACK - 1):
             gather_woven(j)
-        last_plane_in_halves()
-        halves = ((0, HALF), (HALF, S))
-        def rows(i, g, engines, order=(0, 1), slots=(None, None)):
-            spans = halves if i == 2 else ((0, S),)
-            for m in order:
-                weave(i, g, m, engines[m])
-            for m in order:
-                quant(i, g, m, slot=slots[m])
-            for m in order:
-                if (i, m) != (1, 1):
-                    multiply(i, g, m, spans)
+        token_tiles(1)
+        for a, b in HALVES:
+            gather_woven(PACK - 1, a, b)
+        for a, b in HALVES:
+            quantise_tokens(1, a, b)
 
-        rows(0, 0, ("scalar", "scalar"))
-        rows(0, 1, ("vector", "scalar"))
-        rows(1, 0, ("scalar", "vector"), (1, 0))
-        fold(0, 0, slot="woven_100")
-        fold(0, 1, slot="woven_101")
-        rows(1, 1, ("vector", "vector"))
+        prepare(0, 0, (on_scalar, on_scalar))
+        for m in (0, 1):
+            multiply(0, 0, m)
+        prepare(0, 1, (on_vector, on_scalar))
+        for m in (0, 1):
+            multiply(0, 1, m)
+
+        prepare(1, 0, (on_scalar, on_vector), order=(1, 0))
+        multiply(1, 0, 0)
+        keep_first(0, slot="woven_100")
+        keep_first(1, slot="woven_101")
+        prepare(1, 1, (on_vector, on_vector))
+        multiply(1, 1, 0)
         multiply(1, 1, 1, first=1)
         multiply(1, 0, 1, first=1)
-        rows(2, 0, ("vector", "vector"))
-        fold(1, 0, slot="woven_200")
-        weave(2, 1, 0, "scalar")
-        quant(2, 1, 0)
-        multiply(2, 1, 0, halves)
-        fold(1, 1, slot="raw_210")
-        weave(2, 1, 1, "scalar")
-        quant(2, 1, 1)
-        multiply(2, 1, 1, halves)
-        fold(2, 0, 0, HALF)
-        fold(2, 0, HALF, S, slot="woven_211")
-        fold(2, 1, 0, HALF)
-        fold(2, 1, HALF, S)
+
+        prepare(2, 0, (on_vector, on_vector))
+        for m in (0, 1):
+            multiply(2, 0, m, HALVES)
+        max_second(0, slot="woven_200")
+        weave(2, 1, 0, on_scalar)
+        quantise_weights(2, 1, 0)
+        multiply(2, 1, 0, HALVES)
+        max_second(1, slot="raw_210")
+        weave(2, 1, 1, on_scalar)
+        quantise_weights(2, 1, 1)
+        multiply(2, 1, 1, HALVES)
+        max_third_and_store(0, 0, HALF)
+        max_third_and_store(0, HALF, S, slot="woven_211")
+        for a, b in HALVES:
+            max_third_and_store(1, a, b)

@@ -12,11 +12,13 @@ U16 = mybir.dt.uint16
 U8 = mybir.dt.uint8
 FP8X4 = mybir.dt.float8_e4m3fn_x4
 MAX = mybir.AluOpType.max
+COPY = mybir.ActivationFunctionType.Copy
 
 P = 128
 PACK = 4
 KP = P * PACK
 HALF = S // 2
+SPLIT = 384
 GROUP = 16
 PAIR = 2
 ALIGN = 256
@@ -154,8 +156,12 @@ def tile_picked_maxout_max_e_kernel(tc, xT, w1, w2, w3, offs, out):
         for j in range(1, PACK - 1):
             gather_woven(j)
         token_tiles(1)
-        for a, b in HALVES:
-            gather_woven(PACK - 1, a, b)
+        quarter = new_tile([P, S - SPLIT], BF16, "quarter")
+        gather_woven(PACK - 1, 0, SPLIT)
+        nc.scalar.activation(
+            out=quarter[:], in_=planes[1, PACK - 1][:].indirect(offsets[:, SPLIT // GROUP :]), func=COPY
+        )
+        nc.vector.tensor_copy(out=picked[1][:, SPLIT:, PACK - 1], in_=quarter[:])
         for a, b in HALVES:
             quantise_tokens(1, a, b)
 

from contextlib import ExitStack

import concourse.mybir as mybir

K, T, S, N = 1024, 2048, 512, 256
FLOPS = 3 * 2 * K * N * S

F32 = mybir.dt.float32
BF16 = mybir.dt.bfloat16
U32 = mybir.dt.uint32
U16 = mybir.dt.uint16
U8 = mybir.dt.uint8
FP8X4 = mybir.dt.float8_e4m3fn_x4
MAX = mybir.AluOpType.max
COPY = mybir.ActivationFunctionType.Copy

P = 128
PACK = 4
KP = P * PACK
HALF = S // 2
SPLIT = 384
GROUP = 16
PAIR = 2
ALIGN = 256
WHOLE = ((0, S),)
HALVES = ((0, HALF), (HALF, S))


def tile_picked_maxout_max_e_kernel(tc, xT, w1, w2, w3, offs, out):
    nc = tc.nc
    ws = (w1, w2, w3)
    with ExitStack() as ctx:
        keep = ctx.enter_context(tc.tile_pool(name="keep", bufs=1))
        psum = ctx.enter_context(tc.psum_pool(name="psum", bufs=1))

        def new_tile(shape, dtype, name, slot=None):
            return keep.tile(shape, dtype, name=name, tag=slot or name, align_bytes=ALIGN)

        offsets = keep.tile([P, S // GROUP], U16, name="offsets")
        x_rows = xT.rearrange("(g p j) t -> g p j t", p=P, j=PACK)
        planes, raw = {}, {}

        def load_plane(g, j, queue=nc.sync):
            planes[g, j] = new_tile([P, T], F32, f"x_{g}{j}")
            queue.dma_start(out=planes[g, j][:], in_=x_rows[g][:, j, :])

        def load_weights(i, g, tiles):
            cols = slice(tiles[0] * P, (tiles[-1] + 1) * P)
            rows = new_tile([P, PACK, P * len(tiles)], F32, f"raw_{i}{g}{tiles[0]}")
            nc.sync.dma_start(
                out=rows[:], in_=ws[i][g * KP : (g + 1) * KP, cols].rearrange("(p j) n -> p j n", j=PACK)
            )
            for m in tiles:
                raw[i, g, m] = rows[:, :, (m - tiles[0]) * P : (m - tiles[0] + 1) * P]

        picked, x_codes, x_scales = {}, {}, {}
        woven, w_codes, w_scales, acc, best = {}, {}, {}, {}, {}
        dense = {a: new_tile([P, PACK, HALF], F32, f"dense_{a}") for a, b in HALVES}

        def gather_dense(j, a, b):
            nc.vector.tensor_copy(
                out=dense[a][:, j, :], in_=planes[0, j][:].indirect(offsets[:, a // GROUP : b // GROUP])
            )

        def gather_woven(j, a=0, b=S):
            nc.vector.tensor_copy(
                out=picked[1][:, a:b, j], in_=planes[1, j][:].indirect(offsets[:, a // GROUP : b // GROUP])
            )

        def token_tiles(g, slot=None):
            x_codes[g] = new_tile([P, S], U32, f"x_codes_{g}", slot)
            x_scales[g] = new_tile([P, S], U8, f"x_scales_{g}")

        def quantise_tokens(g, a=0, b=S):
            nc.vector.quantize_mx(
                out=x_codes[g][:, a:b].bitcast(FP8X4),
                scales=x_scales[g][:, a:b],
                in_=picked[g][:].rearrange("p s j -> p (s j)")[:, a * PACK : b * PACK],
            )

        def weave(i, g, m, copy):
            woven[i, g, m] = new_tile([P, P * PACK], BF16, f"woven_{i}{g}{m}")
            copy(
                out=woven[i, g, m][:].rearrange("p (c u j) -> p c j u", u=PAIR, j=PACK),
                in_=raw[i, g, m].rearrange("p j (c u) -> p c j u", u=PAIR),
            )

        def quantise_weights(i, g, m):
            w_codes[i, g, m] = new_tile([P, P], U32, f"codes_{i}{g}{m}")
            w_scales[i, g, m] = new_tile([P, P], U8, f"scales_{i}{g}{m}")
            nc.vector.quantize_mx(
                out=w_codes[i, g, m][:].bitcast(FP8X4), scales=w_scales[i, g, m][:], in_=woven[i, g, m][:]
            )

        def multiply(i, g, m, spans=WHOLE, first=0):
            for a, b in spans:
                if g == first:
                    acc[i, m, a] = psum.tile([P, b - a], F32, name=f"acc_{i}{m}_{a}")
                nc.tensor.matmul_mx(
                    out=acc[i, m, a][:],
                    lhsT=w_codes[i, g, m][:].bitcast(FP8X4),
                    lhsT_scale=w_scales[i, g, m][:],
                    rhs=x_codes[g][:, a:b].bitcast(FP8X4),
                    rhs_scale=x_scales[g][:, a:b],
                    start=(g == first),
                    stop=(g != first),
                )

        def prepare(i, g, copies, order=(0, 1)):
            for m in order:
                weave(i, g, m, copies[m])
            for m in order:
                quantise_weights(i, g, m)

        def keep_first(m, slot):
            best[0, m] = new_tile([P, S], F32, f"best_0{m}_0", slot)
            nc.scalar.copy(out=best[0, m][:], in_=acc[0, m, 0][:])

        def max_second(m, slot):
            best[1, m] = new_tile([P, S], F32, f"best_1{m}_0", slot)
            nc.vector.tensor_tensor(out=best[1, m][:], in0=acc[1, m, 0][:], in1=best[0, m][:], op=MAX)

        def max_third_and_store(m, a, b, slot=None):
            result = new_tile([P, b - a], F32, f"best_2{m}_{a}", slot)
            nc.vector.tensor_tensor(out=result[:], in0=acc[2, m, a][:], in1=best[1, m][:, a:b], op=MAX)
            nc.sync.dma_start(out=out[m * P : (m + 1) * P, a:b], in_=result[:])

        on_vector, on_scalar = nc.vector.tensor_copy, nc.scalar.copy

        load_plane(0, 0, nc.scalar)
        load_plane(0, 1)
        nc.sync.dma_start(offsets[:], offs)
        load_plane(0, 2, nc.scalar)
        load_plane(0, 3)
        for j in range(PACK):
            load_plane(1, j)
        for i, g in ((0, 0), (0, 1), (1, 0), (1, 1), (2, 0)):
            load_weights(i, g, (0, 1))
        load_weights(2, 1, (0,))
        load_weights(2, 1, (1,))

        for pair in ((0, 1), (2, 3)):
            for a, b in HALVES:
                for j in pair:
                    gather_dense(j, a, b)
        picked[0] = new_tile([P, S, PACK], BF16, "picked_0")
        for a, b in HALVES:
            nc.scalar.copy(
                out=picked[0][:, a:b, :].rearrange("p (c u) j -> p c j u", u=PAIR),
                in_=dense[a][:].rearrange("p j (c u) -> p c j u", u=PAIR),
            )
        picked[1] = new_tile([P, S, PACK], BF16, "picked_1")
        gather_woven(0)
        token_tiles(0, slot="x_10")
        quantise_tokens(0)
        for j in range(1, PACK - 1):
            gather_woven(j)
        token_tiles(1)
        quarter = new_tile([P, S - SPLIT], BF16, "quarter")
        gather_woven(PACK - 1, 0, SPLIT)
        nc.scalar.activation(
            out=quarter[:], in_=planes[1, PACK - 1][:].indirect(offsets[:, SPLIT // GROUP :]), func=COPY
        )
        nc.vector.tensor_copy(out=picked[1][:, SPLIT:, PACK - 1], in_=quarter[:])
        for a, b in HALVES:
            quantise_tokens(1, a, b)

        prepare(0, 0, (on_scalar, on_scalar))
        for m in (0, 1):
            multiply(0, 0, m)
        prepare(0, 1, (on_vector, on_scalar))
        for m in (0, 1):
            multiply(0, 1, m)

        prepare(1, 0, (on_scalar, on_vector), order=(1, 0))
        multiply(1, 0, 0)
        keep_first(0, slot="woven_100")
        keep_first(1, slot="woven_101")
        prepare(1, 1, (on_vector, on_vector))
        multiply(1, 1, 0)
        multiply(1, 1, 1, first=1)
        multiply(1, 0, 1, first=1)

        prepare(2, 0, (on_vector, on_vector))
        for m in (0, 1):
            multiply(2, 0, m, HALVES)
        max_second(0, slot="woven_200")
        weave(2, 1, 0, on_scalar)
        quantise_weights(2, 1, 0)
        multiply(2, 1, 0, HALVES)
        max_second(1, slot="raw_210")
        weave(2, 1, 1, on_scalar)
        quantise_weights(2, 1, 1)
        multiply(2, 1, 1, HALVES)
        max_third_and_store(0, 0, HALF)
        max_third_and_store(0, HALF, S, slot="woven_211")
        for a, b in HALVES:
            max_third_and_store(1, a, b)
